import numpy as np
import ml_dtypes


def mxq(x, axis, fmt="e4m3"):
    dtype, down = {"e4m3": (ml_dtypes.float8_e4m3fn, 7), "e5m2": (ml_dtypes.float8_e5m2, 14)}[fmt]
    v = np.moveaxis(np.asarray(x, np.float32).astype(ml_dtypes.bfloat16).astype(np.float64), axis, -1)
    blocks = v.reshape(v.shape[:-1] + (-1, 32))
    amax = np.abs(blocks).max(-1, keepdims=True)
    byte = np.maximum(np.where(amax > 0, np.frexp(amax)[1] - 1 + 127, 0) - down, 1)
    scale = np.exp2(byte - 127.0)
    codes = (blocks / scale).astype(np.float32).astype(dtype).astype(np.float64)
    return np.moveaxis((codes * scale).reshape(v.shape), -1, axis)


WIDE = False


def mx_kscale(k):
    if not WIDE:
        return np.ones(k)
    levels = np.array([10, -10, 5, -5, 0])
    if k % 512:
        return np.exp2(np.random.permutation(np.resize(levels, k // 32))).repeat(32)
    a = np.empty((k // 512, 16))
    for p in range(k // 512):
        a[p, :8] = np.random.permutation(np.resize(levels, 8))
        for g in range(8):
            far = levels[np.abs(levels - a[p, g]) >= 10]
            a[p, g + 8] = far[np.random.randint(len(far))]
    return np.exp2(a.ravel()).repeat(32)


def f64(x):
    return np.asarray(x).astype(np.float64)


E2M1 = np.array([0.0, 0.5, 1.0, 1.5, 2.0, 3.0, 4.0, 6.0, -0.0, -0.5, -1.0, -1.5, -2.0, -3.0, -4.0, -6.0])


def pack_weight(w, fmt):
    k, n = w.shape
    w = f64(np.asarray(w, np.float32).astype(ml_dtypes.bfloat16)).reshape(k // 32, 32, n)
    amax = np.abs(w).max(1)
    if fmt == "e4m3":
        byte = np.frexp(amax)[1] - 1 + 127 - 7
    else:
        mant, ex = np.frexp(amax / 6.0)
        byte = np.where(mant > 0.5, ex, ex - 1) + 127
    byte = np.clip(np.where(amax > 0, byte, 1), 1, 254)
    scaled = (w * np.exp2(127.0 - byte)[:, None, :]).reshape(k, n).astype(np.float32)
    by_word = np.ascontiguousarray(scaled.reshape(k // 512, 128, 4, n).transpose(0, 1, 3, 2))
    if fmt == "e4m3":
        words = by_word.astype(ml_dtypes.float8_e4m3fn).view(np.uint8)
    else:
        c = by_word.astype(ml_dtypes.float4_e2m1fn).view(np.uint8) & 0xF
        words = (c[..., 0::2] | (c[..., 1::2] << 4)).reshape(k // 512, 128, 2 * n)
    return np.ascontiguousarray(words), np.ascontiguousarray(byte.astype(np.uint8).reshape(k // 512, 16, n))


def unpack_weight(words, scales, fmt):
    g, _, n = scales.shape
    words = np.ascontiguousarray(words).reshape(g, 128, n, -1)
    if fmt == "e4m3":
        vals = words.view(ml_dtypes.float8_e4m3fn).astype(np.float64)
    else:
        nib = np.empty((g, 128, n, 4), np.uint8)
        nib[..., 0::2] = words & 0xF
        nib[..., 1::2] = words >> 4
        vals = E2M1[nib]
    vals = vals * np.repeat(np.exp2(scales.astype(np.float64) - 127.0), 8, axis=1)[..., None]
    return vals.transpose(0, 1, 3, 2).reshape(g * 512, n)


def bf(x):
    return np.asarray(x, np.float32).astype(ml_dtypes.bfloat16)


def planes(Y):
    r, m = Y.shape
    b = f64(bf(Y)).reshape(r // 32, 32, m)
    amax = np.abs(b).max(1)
    byte = np.clip(np.where(amax > 0, np.frexp(amax)[1] - 1 + 127 - 7, 1), 1, 254)
    codes = (b * np.exp2(127.0 - byte)[:, None, :]).reshape(r, m).astype(np.float32).astype(ml_dtypes.float8_e4m3fn).view(np.uint8)
    words = codes.reshape(r // 512, 128, 4, m).transpose(0, 1, 3, 2)
    return np.ascontiguousarray(words), np.ascontiguousarray(byte.astype(np.uint8).reshape(r // 512, 16, m))


K, L, Q, I = 512, 512, 512, 1024


def setup_inputs():
    n = np.random.standard_normal
    fk = mx_kscale(K)
    fl = mx_kscale(L)
    qap = pack_weight(n((K, Q)) * 0.03 * fk[:, None], "e2m1")
    kap = pack_weight(n((K, I)) / fk[:, None], "e4m3")
    kbp = pack_weight(n((L, I)) / fl[:, None], "e2m1")
    return {
        "qa_words": qap[0],
        "qa_scales": qap[1],
        "ka_words": kap[0],
        "ka_scales": kap[1],
        "qb": (n((L, Q)) * 0.03 * fl[:, None]).astype(np.float32),
        "kb_words": kbp[0],
        "kb_scales": kbp[1],
        "cw1": (np.random.uniform(0.5, 2.0, (1, I))).astype(np.float32),
    }


def reference(qa_words, qa_scales, ka_words, ka_scales, qb, kb_words, kb_scales, cw1):
    qau = unpack_weight(qa_words, qa_scales, "e2m1")
    kau = unpack_weight(ka_words, ka_scales, "e4m3")
    kbu = unpack_weight(kb_words, kb_scales, "e2m1")
    qbq = mxq(f64(qb), 0, "e4m3")
    a = qau.T @ kau + qbq.T @ kbu
    e = np.exp(a)
    y = 256.0 * e * f64(cw1) / np.sum(e, axis=1, keepdims=True)
    words, scales = planes(y)
    return y, words, scales

@@ -1,0 +1,244 @@
+from contextlib import ExitStack
+
+import concourse.mybir as mybir
+from concourse.masks import make_identity
+
+K, L, Q, I = 512, 512, 512, 1024
+FLOPS = 2 * (K + L) * Q * I
+
+F32 = mybir.dt.float32
+BF16 = mybir.dt.bfloat16
+I32 = mybir.dt.int32
+U32 = mybir.dt.uint32
+U8 = mybir.dt.uint8
+FP8X4 = mybir.dt.float8_e4m3fn_x4
+FP4X4 = mybir.dt.float4_e2m1fn_x4
+ALU = mybir.AluOpType
+ACT = mybir.ActivationFunctionType
+
+P = 128
+PACK = 4
+BANK = 512
+CHUNK = 256
+SCORE_BANKS = 6
+QB_HALF = Q // 2
+QB_VECTOR_GROUPS = 44
+
+
+def tile_mix_shares_from_two_sources_pl_kernel(
+    tc, qa_words, qa_scales, ka_words, ka_scales, qb, kb_words, kb_scales, cw1, out_0, out_1, out_2
+):
+    nc = tc.nc
+    with ExitStack() as ctx:
+        sb = ctx.enter_context(tc.tile_pool(name="sb", bufs=1))
+        ps = ctx.enter_context(tc.psum_pool(name="ps", bufs=1))
+        ctx.enter_context(tc.manual_schedule())
+
+        qa_raw = sb.tile([P, 2 * Q], U8, align_bytes=64)
+        qa_raw_scale = sb.tile([P, Q], U8, align_bytes=64)
+        qa_codes = sb.tile([P, 2 * Q], U8, align_bytes=64)
+        qa_scale = sb.tile([P, Q], U8, align_bytes=64)
+        ka_codes = sb.tile([P, I], U32, align_bytes=64)
+        ka_scale = sb.tile([P, I], U8, align_bytes=64)
+        kb_codes = sb.tile([P, 2 * I], U8, align_bytes=64)
+        kb_scale = sb.tile([P, I], U8, align_bytes=64)
+        qb_raw = [sb.tile([P, PACK, QB_HALF], F32, name="qb_raw%d" % u, align_bytes=64) for u in range(2)]
+        qb_bf = sb.tile([P, PACK * Q], BF16, align_bytes=64)
+        qb_codes = sb.tile([P, Q], U32, align_bytes=64)
+        qb_scale = sb.tile([P, Q], U8, align_bytes=64)
+        cw_rows = sb.tile([P, 2, PACK], F32)
+        cw_256 = sb.tile([P, 2 * PACK], F32)
+        ident = sb.tile([P, P], F32)
+        warm_in = sb.tile([P, 1], F32)
+        warm_out = sb.tile([P, 1], F32)
+
+        def load_scales(queue, plane, scales):
+            for quad in range(4):
+                queue.dma_start(
+                    out=plane[32 * quad : 32 * quad + 4, :].bitcast(I32),
+                    in_=scales[0, 4 * quad : 4 * quad + 4, :].bitcast(I32),
+                )
+
+        qb_rows = qb.rearrange("(p j) q -> p j q", j=PACK)
+
+        nc.vector.memset(qa_raw_scale[:].bitcast(I32), 0)
+        nc.vector.memset(ka_scale[:].bitcast(I32), 0)
+        nc.gpsimd.memset(warm_in[:], 0.0)
+        nc.gpsimd.memset(kb_scale[:].bitcast(I32), 0)
+        nc.scalar.activation(out=warm_out[:], in_=warm_in[:], func=ACT.Exp)
+
+        nc.sync.dma_start(out=qb_raw[0][:], in_=qb_rows[:, :, 0:QB_HALF])
+        nc.sync.dma_start(out=qa_raw[:].bitcast(I32), in_=qa_words[0].bitcast(I32))
+        load_scales(nc.sync, qa_raw_scale, qa_scales)
+        nc.sync.dma_start(
+            out=ka_codes[:].bitcast(I32), in_=ka_words[0].rearrange("p n t -> p (n t)").bitcast(I32)
+        )
+        nc.sync.dma_start(out=qb_raw[1][:], in_=qb_rows[:, :, QB_HALF:Q])
+        nc.sync.dma_start(out=kb_codes[:].bitcast(I32), in_=kb_words[0].bitcast(I32))
+        load_scales(nc.scalar, ka_scale, ka_scales)
+        nc.sync.dma_start(out=cw_rows[:], in_=cw1[0].rearrange("(h n m) -> n h m", h=2, m=PACK))
+        load_scales(nc.gpsimd, kb_scale, kb_scales)
+        make_identity(nc, ident[:])
+        nc.gpsimd.tensor_scalar(
+            out=cw_256[:], in0=cw_rows[:].rearrange("p h m -> p (h m)"),
+            scalar1=256.0, scalar2=0.0, op0=ALU.mult, op1=ALU.add,
+        )
+
+        qb_dealt = qb_bf[:].rearrange("p (r m j) -> p m r j", r=PACK, j=PACK)
+        half_groups = QB_HALF // PACK
+
+        def round_qb(copy, u, lo, hi):
+            src = qb_raw[u][:].rearrange("p j (m r) -> p m r j", r=PACK)
+            copy(out=qb_dealt[:, u * half_groups + lo : u * half_groups + hi], in_=src[:, lo:hi])
+
+        round_qb(nc.vector.tensor_copy, 0, 0, half_groups)
+        nc.vector.tensor_copy(
+            out=qa_codes[:].rearrange("p (r m b) -> p r m b", r=PACK, b=2),
+            in_=qa_raw[:].rearrange("p (m r b) -> p r m b", r=PACK, b=2),
+        )
+        nc.vector.tensor_copy(
+            out=qa_scale[:].rearrange("p (r m) -> p r m", r=PACK),
+            in_=qa_raw_scale[:].rearrange("p (m r) -> p r m", r=PACK),
+        )
+        round_qb(nc.vector.tensor_copy, 1, 0, QB_VECTOR_GROUPS)
+        round_qb(nc.scalar.copy, 1, QB_VECTOR_GROUPS, half_groups)
+        for r in range(PACK):
+            nc.vector.quantize_mx(
+                out=qb_codes[:, P * r : P * (r + 1)].bitcast(FP8X4),
+                scales=qb_scale[:, P * r : P * (r + 1)],
+                in_=qb_bf[:, PACK * P * r : PACK * P * (r + 1)],
+            )
+
+        order = [(0, 0), (1, 0), (0, 1), (2, 0), (1, 1), (3, 0), (2, 1), (3, 1)]
+        acc = {}
+
+        def pass_a(n):
+            r, h = order[n]
+            acc[n] = ps.tile([P, BANK], F32, name="acc%d" % n, tag="acc%d" % (n % SCORE_BANKS))
+            nc.tensor.matmul_mx(
+                out=acc[n][:],
+                lhsT=qa_codes[:, 2 * P * r : 2 * P * (r + 1)].bitcast(FP4X4),
+                lhsT_scale=qa_scale[:, P * r : P * (r + 1)],
+                rhs=ka_codes[:, BANK * h : BANK * (h + 1)].bitcast(FP8X4),
+                rhs_scale=ka_scale[:, BANK * h : BANK * (h + 1)],
+                start=True, stop=False,
+            )
+
+        def pass_b(n):
+            r, h = order[n]
+            nc.tensor.matmul_mx(
+                out=acc[n][:],
+                lhsT=qb_codes[:, P * r : P * (r + 1)].bitcast(FP8X4),
+                lhsT_scale=qb_scale[:, P * r : P * (r + 1)],
+                rhs=kb_codes[:, 2 * BANK * h : 2 * BANK * (h + 1)].bitcast(FP4X4),
+                rhs_scale=kb_scale[:, BANK * h : BANK * (h + 1)],
+                start=False, stop=True,
+            )
+
+        neg = [sb.tile([P, I], F32, name="neg%d" % r) for r in range(PACK)]
+        expd = [sb.tile([P, I], F32, name="expd%d" % r) for r in range(PACK)]
+        low_half = [sb.tile([P, 1], F32, name="low_half%d" % r) for r in range(PACK)]
+        low_row = [sb.tile([P, 1], F32, name="low_row%d" % r) for r in range(PACK)]
+        total = [sb.tile([P, 1], F32, name="total%d" % r) for r in range(PACK)]
+        inv = [sb.tile([P, 1], F32, name="inv%d" % r) for r in range(PACK)]
+        y = [sb.tile([P, PACK, BANK], F32, name="y%d" % h) for h in range(2)]
+        y_bf = [sb.tile([P, PACK * CHUNK], BF16, name="y_bf%d" % c, align_bytes=64) for c in range(4)]
+        y_codes = [sb.tile([P, CHUNK], U32, name="y_codes%d" % c, align_bytes=64) for c in range(4)]
+        y_scale = sb.tile([P, I], U8, align_bytes=64)
+        cw_bank = [ps.tile([P, BANK], F32, name="cw_bank%d" % h) for h in range(2)]
+
+        def drain(n):
+            r, h = order[n]
+            nc.vector.tensor_scalar(
+                out=neg[r][:, BANK * h : BANK * (h + 1)], in0=acc[n][:],
+                scalar1=-1.0, scalar2=None if h == 0 else low_half[r][:],
+                op0=ALU.mult, op1=ALU.min,
+                accum_out=low_half[r][:] if h == 0 else low_row[r][:],
+            )
+            if h == 1:
+                nc.scalar.activation(
+                    out=expd[r][:], in_=neg[r][:], func=ACT.Exp,
+                    bias=low_row[r][:], scale=-1.0, accum_out=total[r][:],
+                )
+
+        def invert(r):
+            nc.vector.reciprocal(out=inv[r][:], in_=total[r][:])
+
+        out_rows = out_0.rearrange("(p r) i -> p r i", r=PACK)
+
+        def share(r, h, lo=0, hi=BANK):
+            nc.vector.scalar_tensor_tensor(
+                out=y[h][:, r, lo:hi], in0=expd[r][:, BANK * h + lo : BANK * h + hi],
+                scalar=inv[r][:], in1=cw_bank[h][:, lo:hi], op0=ALU.mult, op1=ALU.mult,
+            )
+            if hi == BANK:
+                nc.sync.dma_start(out=out_rows[:, r, BANK * h : BANK * (h + 1)], in_=y[h][:, r, :])
+
+        def round_y(copy, c):
+            h, lo = divmod(CHUNK * c, BANK)
+            copy(
+                out=y_bf[c][:].rearrange("p (g i r) -> p g r i", i=4, r=PACK),
+                in_=y[h][:, :, lo : lo + CHUNK].rearrange("p r (g i) -> p g r i", i=4),
+            )
+
+        code_words = out_1[0].rearrange("p c t -> p (c t)").bitcast(I32)
+
+        def quantize_y(c):
+            nc.vector.quantize_mx(
+                out=y_codes[c][:].bitcast(FP8X4),
+                scales=y_scale[:, CHUNK * c : CHUNK * (c + 1)],
+                in_=y_bf[c][:],
+            )
+            nc.sync.dma_start(out=code_words[:, CHUNK * c : CHUNK * (c + 1)], in_=y_codes[c][:].bitcast(I32))
+
+        for n in range(2):
+            pass_a(n)
+        for n in range(2):
+            pass_b(n)
+        for n in range(2, SCORE_BANKS):
+            pass_a(n)
+            pass_b(n)
+        for n in range(SCORE_BANKS, 8):
+            drain(n - SCORE_BANKS)
+            pass_a(n)
+            pass_b(n)
+        for h in range(2):
+            for m in range(PACK):
+                col = PACK * h + m
+                nc.tensor.transpose(
+                    out=cw_bank[h][:].rearrange("p (n m) -> p m n", m=PACK)[:, m, :],
+                    in_=cw_256[:, col : col + 1].to_broadcast([P, P]),
+                    identity=ident[:],
+                )
+        for n in range(2, 6):
+            drain(n)
+        invert(0)
+        drain(6)
+        drain(7)
+        invert(1)
+        share(0, 0)
+        invert(2)
+        share(1, 0)
+        share(2, 0)
+        invert(3)
+        share(0, 1)
+        share(3, 0, 0, CHUNK)
+        round_y(nc.scalar.copy, 0)
+        share(3, 0, CHUNK, BANK)
+        round_y(nc.scalar.copy, 1)
+        share(1, 1)
+        share(2, 1)
+        share(3, 1, 0, CHUNK)
+        round_y(nc.scalar.copy, 2)
+        share(3, 1, CHUNK, BANK)
+        quantize_y(0)
+        round_y(nc.vector.tensor_copy, 3)
+        quantize_y(1)
+        quantize_y(3)
+        quantize_y(2)
+        for quad in range(4):
+            queue = nc.scalar if quad % 2 == 0 else nc.sync
+            queue.dma_start(
+                out=out_2[0, 4 * quad : 4 * quad + 4, :].bitcast(I32),
+                in_=y_scale[32 * quad : 32 * quad + 4, :].bitcast(I32),
+            )

@@ -38,7 +38,7 @@ def tile_mix_shares_from_two_sources_pl_kernel(
         qa_raw_scale = sb.tile([P, Q], U8, align_bytes=64)
         qa_codes = sb.tile([P, 2 * Q], U8, align_bytes=64)
         qa_scale = sb.tile([P, Q], U8, align_bytes=64)
-        ka_codes = sb.tile([P, I], U32, align_bytes=64)
+        ka_codes = [sb.tile([P, BANK], U32, name="ka_codes%d" % h, align_bytes=64) for h in range(2)]
         ka_scale = sb.tile([P, I], U8, align_bytes=64)
         kb_codes = sb.tile([P, 2 * I], U8, align_bytes=64)
         kb_scale = sb.tile([P, I], U8, align_bytes=64)
@@ -61,28 +61,26 @@ def tile_mix_shares_from_two_sources_pl_kernel(
 
         qb_rows = qb.rearrange("(p j) q -> p j q", j=PACK)
 
+        ka_flat = ka_words[0].rearrange("p n t -> p (n t)").bitcast(I32)
+
         nc.vector.memset(qa_raw_scale[:].bitcast(I32), 0)
+        nc.vector.memset(ident[:], 0.0)
         nc.vector.memset(ka_scale[:].bitcast(I32), 0)
         nc.gpsimd.memset(warm_in[:], 0.0)
-        nc.gpsimd.memset(kb_scale[:].bitcast(I32), 0)
+        nc.vector.memset(kb_scale[:].bitcast(I32), 0)
         nc.scalar.activation(out=warm_out[:], in_=warm_in[:], func=ACT.Exp)
+        nc.gpsimd.dma_start(out=cw_rows[:], in_=cw1[0].rearrange("(h n m) -> n h m", h=2, m=PACK))
+        make_identity(nc, ident[:], nomemset=True)
 
-        nc.sync.dma_start(out=qb_raw[0][:], in_=qb_rows[:, :, 0:QB_HALF])
         nc.sync.dma_start(out=qa_raw[:].bitcast(I32), in_=qa_words[0].bitcast(I32))
         load_scales(nc.sync, qa_raw_scale, qa_scales)
-        nc.sync.dma_start(
-            out=ka_codes[:].bitcast(I32), in_=ka_words[0].rearrange("p n t -> p (n t)").bitcast(I32)
-        )
+        nc.sync.dma_start(out=ka_codes[0][:].bitcast(I32), in_=ka_flat[:, 0:BANK])
+        nc.sync.dma_start(out=qb_raw[0][:], in_=qb_rows[:, :, 0:QB_HALF])
+        load_scales(nc.sync, ka_scale, ka_scales)
         nc.sync.dma_start(out=qb_raw[1][:], in_=qb_rows[:, :, QB_HALF:Q])
         nc.sync.dma_start(out=kb_codes[:].bitcast(I32), in_=kb_words[0].bitcast(I32))
-        load_scales(nc.scalar, ka_scale, ka_scales)
-        nc.sync.dma_start(out=cw_rows[:], in_=cw1[0].rearrange("(h n m) -> n h m", h=2, m=PACK))
-        load_scales(nc.gpsimd, kb_scale, kb_scales)
-        make_identity(nc, ident[:])
-        nc.gpsimd.tensor_scalar(
-            out=cw_256[:], in0=cw_rows[:].rearrange("p h m -> p (h m)"),
-            scalar1=256.0, scalar2=0.0, op0=ALU.mult, op1=ALU.add,
-        )
+        load_scales(nc.sync, kb_scale, kb_scales)
+        nc.sync.dma_start(out=ka_codes[1][:].bitcast(I32), in_=ka_flat[:, BANK:I])
 
         qb_dealt = qb_bf[:].rearrange("p (r m j) -> p m r j", r=PACK, j=PACK)
         half_groups = QB_HALF // PACK
@@ -91,7 +89,6 @@ def tile_mix_shares_from_two_sources_pl_kernel(
             src = qb_raw[u][:].rearrange("p j (m r) -> p m r j", r=PACK)
             copy(out=qb_dealt[:, u * half_groups + lo : u * half_groups + hi], in_=src[:, lo:hi])
 
-        round_qb(nc.vector.tensor_copy, 0, 0, half_groups)
         nc.vector.tensor_copy(
             out=qa_codes[:].rearrange("p (r m b) -> p r m b", r=PACK, b=2),
             in_=qa_raw[:].rearrange("p (m r b) -> p r m b", r=PACK, b=2),
@@ -99,6 +96,13 @@ def tile_mix_shares_from_two_sources_pl_kernel(
         nc.vector.tensor_copy(
             out=qa_scale[:].rearrange("p (r m) -> p r m", r=PACK),
             in_=qa_raw_scale[:].rearrange("p (m r) -> p r m", r=PACK),
+        )
+        cw_bank = [ps.tile([P, BANK], F32, name="cw_bank%d" % h) for h in range(2)]
+
+        round_qb(nc.vector.tensor_copy, 0, 0, half_groups)
+        nc.vector.tensor_scalar(
+            out=cw_256[:], in0=cw_rows[:].rearrange("p h m -> p (h m)"),
+            scalar1=256.0, scalar2=None, op0=ALU.mult,
         )
         round_qb(nc.vector.tensor_copy, 1, 0, QB_VECTOR_GROUPS)
         round_qb(nc.scalar.copy, 1, QB_VECTOR_GROUPS, half_groups)
@@ -119,7 +123,7 @@ def tile_mix_shares_from_two_sources_pl_kernel(
                 out=acc[n][:],
                 lhsT=qa_codes[:, 2 * P * r : 2 * P * (r + 1)].bitcast(FP4X4),
                 lhsT_scale=qa_scale[:, P * r : P * (r + 1)],
-                rhs=ka_codes[:, BANK * h : BANK * (h + 1)].bitcast(FP8X4),
+                rhs=ka_codes[h][:].bitcast(FP8X4),
                 rhs_scale=ka_scale[:, BANK * h : BANK * (h + 1)],
                 start=True, stop=False,
             )
@@ -145,7 +149,6 @@ def tile_mix_shares_from_two_sources_pl_kernel(
         y_bf = [sb.tile([P, PACK * CHUNK], BF16, name="y_bf%d" % c, align_bytes=64) for c in range(4)]
         y_codes = [sb.tile([P, CHUNK], U32, name="y_codes%d" % c, align_bytes=64) for c in range(4)]
         y_scale = sb.tile([P, I], U8, align_bytes=64)
-        cw_bank = [ps.tile([P, BANK], F32, name="cw_bank%d" % h) for h in range(2)]
 
         def drain(n):
             r, h = order[n]
@@ -191,13 +194,17 @@ def tile_mix_shares_from_two_sources_pl_kernel(
             )
             nc.sync.dma_start(out=code_words[:, CHUNK * c : CHUNK * (c + 1)], in_=y_codes[c][:].bitcast(I32))
 
-        for n in range(2):
+        for n in (0, 1, 3):
             pass_a(n)
-        for n in range(2):
-            pass_b(n)
-        for n in range(2, SCORE_BANKS):
-            pass_a(n)
-            pass_b(n)
+        pass_b(0)
+        pass_b(1)
+        pass_a(2)
+        pass_b(2)
+        pass_b(3)
+        pass_a(4)
+        pass_b(4)
+        pass_a(5)
+        pass_b(5)
         for n in range(SCORE_BANKS, 8):
             drain(n - SCORE_BANKS)
             pass_a(n)

@@ -23,6 +23,7 @@ CHUNK = 256
 SCORE_BANKS = 6
 QB_HALF = Q // 2
 QB_VECTOR_GROUPS = 44
+WARM_PASSES = 4
 
 
 def tile_mix_shares_from_two_sources_pl_kernel(
@@ -52,8 +53,8 @@ def tile_mix_shares_from_two_sources_pl_kernel(
         warm_in = sb.tile([P, 1], F32)
         warm_out = sb.tile([P, 1], F32)
 
-        def load_scales(queue, plane, scales):
-            for quad in range(4):
+        def load_scales(queue, plane, scales, quads=range(4)):
+            for quad in quads:
                 queue.dma_start(
                     out=plane[32 * quad : 32 * quad + 4, :].bitcast(I32),
                     in_=scales[0, 4 * quad : 4 * quad + 4, :].bitcast(I32),
@@ -64,22 +65,23 @@ def tile_mix_shares_from_two_sources_pl_kernel(
         ka_flat = ka_words[0].rearrange("p n t -> p (n t)").bitcast(I32)
 
         nc.vector.memset(qa_raw_scale[:].bitcast(I32), 0)
-        nc.vector.memset(ident[:], 0.0)
         nc.vector.memset(ka_scale[:].bitcast(I32), 0)
+        nc.vector.memset(ident[:], 0.0)
         nc.gpsimd.memset(warm_in[:], 0.0)
-        nc.vector.memset(kb_scale[:].bitcast(I32), 0)
+        nc.gpsimd.memset(kb_scale[:].bitcast(I32), 0)
         nc.scalar.activation(out=warm_out[:], in_=warm_in[:], func=ACT.Exp)
+        load_scales(nc.gpsimd, kb_scale, kb_scales, range(1, 4))
         nc.gpsimd.dma_start(out=cw_rows[:], in_=cw1[0].rearrange("(h n m) -> n h m", h=2, m=PACK))
         make_identity(nc, ident[:], nomemset=True)
 
         nc.sync.dma_start(out=qa_raw[:].bitcast(I32), in_=qa_words[0].bitcast(I32))
-        load_scales(nc.sync, qa_raw_scale, qa_scales)
         nc.sync.dma_start(out=ka_codes[0][:].bitcast(I32), in_=ka_flat[:, 0:BANK])
+        load_scales(nc.sync, qa_raw_scale, qa_scales)
         nc.sync.dma_start(out=qb_raw[0][:], in_=qb_rows[:, :, 0:QB_HALF])
-        load_scales(nc.sync, ka_scale, ka_scales)
         nc.sync.dma_start(out=qb_raw[1][:], in_=qb_rows[:, :, QB_HALF:Q])
+        load_scales(nc.sync, ka_scale, ka_scales)
         nc.sync.dma_start(out=kb_codes[:].bitcast(I32), in_=kb_words[0].bitcast(I32))
-        load_scales(nc.sync, kb_scale, kb_scales)
+        load_scales(nc.sync, kb_scale, kb_scales, range(1))
         nc.sync.dma_start(out=ka_codes[1][:].bitcast(I32), in_=ka_flat[:, BANK:I])
 
         qb_dealt = qb_bf[:].rearrange("p (r m j) -> p m r j", r=PACK, j=PACK)
@@ -100,10 +102,6 @@ def tile_mix_shares_from_two_sources_pl_kernel(
         cw_bank = [ps.tile([P, BANK], F32, name="cw_bank%d" % h) for h in range(2)]
 
         round_qb(nc.vector.tensor_copy, 0, 0, half_groups)
-        nc.vector.tensor_scalar(
-            out=cw_256[:], in0=cw_rows[:].rearrange("p h m -> p (h m)"),
-            scalar1=256.0, scalar2=None, op0=ALU.mult,
-        )
         round_qb(nc.vector.tensor_copy, 1, 0, QB_VECTOR_GROUPS)
         round_qb(nc.scalar.copy, 1, QB_VECTOR_GROUPS, half_groups)
         for r in range(PACK):
@@ -112,6 +110,9 @@ def tile_mix_shares_from_two_sources_pl_kernel(
                 scales=qb_scale[:, P * r : P * (r + 1)],
                 in_=qb_bf[:, PACK * P * r : PACK * P * (r + 1)],
             )
+        nc.scalar.activation(
+            out=cw_256[:], in_=cw_rows[:].rearrange("p h m -> p (h m)"), func=ACT.Copy, scale=256.0
+        )
 
         order = [(0, 0), (1, 0), (0, 1), (2, 0), (1, 1), (3, 0), (2, 1), (3, 1)]
         acc = {}
@@ -147,7 +148,7 @@ def tile_mix_shares_from_two_sources_pl_kernel(
         inv = [sb.tile([P, 1], F32, name="inv%d" % r) for r in range(PACK)]
         y = [sb.tile([P, PACK, BANK], F32, name="y%d" % h) for h in range(2)]
         y_bf = [sb.tile([P, PACK * CHUNK], BF16, name="y_bf%d" % c, align_bytes=64) for c in range(4)]
-        y_codes = [sb.tile([P, CHUNK], U32, name="y_codes%d" % c, align_bytes=64) for c in range(4)]
+        y_codes = [sb.tile([P, BANK], U32, name="y_codes%d" % h, align_bytes=64) for h in range(2)]
         y_scale = sb.tile([P, I], U8, align_bytes=64)
 
         def drain(n):
@@ -177,24 +178,36 @@ def tile_mix_shares_from_two_sources_pl_kernel(
             if hi == BANK:
                 nc.sync.dma_start(out=out_rows[:, r, BANK * h : BANK * (h + 1)], in_=y[h][:, r, :])
 
-        def round_y(copy, c):
+        def round_y(copy, c, first=0, last=CHUNK):
             h, lo = divmod(CHUNK * c, BANK)
             copy(
-                out=y_bf[c][:].rearrange("p (g i r) -> p g r i", i=4, r=PACK),
-                in_=y[h][:, :, lo : lo + CHUNK].rearrange("p r (g i) -> p g r i", i=4),
+                out=y_bf[c][:, PACK * first : PACK * last].rearrange("p (g i r) -> p g r i", i=4, r=PACK),
+                in_=y[h][:, :, lo + first : lo + last].rearrange("p r (g i) -> p g r i", i=4),
             )
 
         code_words = out_1[0].rearrange("p c t -> p (c t)").bitcast(I32)
 
         def quantize_y(c):
+            h, lo = divmod(CHUNK * c, BANK)
             nc.vector.quantize_mx(
-                out=y_codes[c][:].bitcast(FP8X4),
+                out=y_codes[h][:, lo : lo + CHUNK].bitcast(FP8X4),
                 scales=y_scale[:, CHUNK * c : CHUNK * (c + 1)],
                 in_=y_bf[c][:],
             )
-            nc.sync.dma_start(out=code_words[:, CHUNK * c : CHUNK * (c + 1)], in_=y_codes[c][:].bitcast(I32))
 
-        for n in (0, 1, 3):
+        def store_codes(h, lo, hi):
+            nc.sync.dma_start(
+                out=code_words[:, BANK * h + lo : BANK * h + hi], in_=y_codes[h][:, lo:hi].bitcast(I32)
+            )
+
+        for n in range(WARM_PASSES):
+            nc.tensor.matmul_mx(
+                out=cw_bank[n % 2][:],
+                lhsT=qa_raw[:, 0 : 2 * P].bitcast(FP4X4), lhsT_scale=qa_raw_scale[:, 0:P],
+                rhs=ka_codes[0][:].bitcast(FP8X4), rhs_scale=qa_raw_scale[:],
+                start=True, stop=True,
+            )
+        for n in (0, 1, 3, 5):
             pass_a(n)
         pass_b(0)
         pass_b(1)
@@ -203,7 +216,6 @@ def tile_mix_shares_from_two_sources_pl_kernel(
         pass_b(3)
         pass_a(4)
         pass_b(4)
-        pass_a(5)
         pass_b(5)
         for n in range(SCORE_BANKS, 8):
             drain(n - SCORE_BANKS)
@@ -228,11 +240,12 @@ def tile_mix_shares_from_two_sources_pl_kernel(
         share(1, 0)
         share(2, 0)
         invert(3)
-        share(0, 1)
+        share(0, 1, 0, CHUNK)
         share(3, 0, 0, CHUNK)
         round_y(nc.scalar.copy, 0)
         share(3, 0, CHUNK, BANK)
         round_y(nc.scalar.copy, 1)
+        share(0, 1, CHUNK, BANK)
         share(1, 1)
         share(2, 1)
         share(3, 1, 0, CHUNK)
@@ -241,8 +254,11 @@ def tile_mix_shares_from_two_sources_pl_kernel(
         quantize_y(0)
         round_y(nc.vector.tensor_copy, 3)
         quantize_y(1)
+        store_codes(0, 0, BANK)
         quantize_y(3)
+        store_codes(1, CHUNK, BANK)
         quantize_y(2)
+        store_codes(1, 0, CHUNK)
         for quad in range(4):
             queue = nc.scalar if quad % 2 == 0 else nc.sync
             queue.dma_start(

@@ -23,7 +23,6 @@ CHUNK = 256
 SCORE_BANKS = 6
 QB_HALF = Q // 2
 QB_VECTOR_GROUPS = 44
-WARM_PASSES = 4
 
 
 def tile_mix_shares_from_two_sources_pl_kernel(
@@ -47,14 +46,12 @@ def tile_mix_shares_from_two_sources_pl_kernel(
         qb_bf = sb.tile([P, PACK * Q], BF16, align_bytes=64)
         qb_codes = sb.tile([P, Q], U32, align_bytes=64)
         qb_scale = sb.tile([P, Q], U8, align_bytes=64)
-        cw_rows = sb.tile([P, 2, PACK], F32)
-        cw_256 = sb.tile([P, 2 * PACK], F32)
+        cw_rows = [sb.tile([P, PACK], F32, name="cw_rows%d" % h) for h in range(2)]
+        cw_256 = [sb.tile([P, PACK], F32, name="cw_256_%d" % h) for h in range(2)]
         ident = sb.tile([P, P], F32)
-        warm_in = sb.tile([P, 1], F32)
-        warm_out = sb.tile([P, 1], F32)
 
-        def load_scales(queue, plane, scales, quads=range(4)):
-            for quad in quads:
+        def load_scales(queue, plane, scales):
+            for quad in range(4):
                 queue.dma_start(
                     out=plane[32 * quad : 32 * quad + 4, :].bitcast(I32),
                     in_=scales[0, 4 * quad : 4 * quad + 4, :].bitcast(I32),
@@ -67,22 +64,28 @@ def tile_mix_shares_from_two_sources_pl_kernel(
         nc.vector.memset(qa_raw_scale[:].bitcast(I32), 0)
         nc.vector.memset(ka_scale[:].bitcast(I32), 0)
         nc.vector.memset(ident[:], 0.0)
-        nc.gpsimd.memset(warm_in[:], 0.0)
-        nc.gpsimd.memset(kb_scale[:].bitcast(I32), 0)
-        nc.scalar.activation(out=warm_out[:], in_=warm_in[:], func=ACT.Exp)
-        load_scales(nc.gpsimd, kb_scale, kb_scales, range(1, 4))
-        nc.gpsimd.dma_start(out=cw_rows[:], in_=cw1[0].rearrange("(h n m) -> n h m", h=2, m=PACK))
+        nc.vector.memset(kb_scale[:].bitcast(I32), 0)
         make_identity(nc, ident[:], nomemset=True)
 
+        def load_weights(h):
+            nc.sync.dma_start(
+                out=cw_rows[h][:], in_=cw1[0, BANK * h : BANK * (h + 1)].rearrange("(n m) -> n m", m=PACK)
+            )
+            nc.gpsimd.tensor_scalar(
+                out=cw_256[h][:], in0=cw_rows[h][:], scalar1=256.0, scalar2=0.0, op0=ALU.mult, op1=ALU.add
+            )
+
+        load_weights(0)
         nc.sync.dma_start(out=qa_raw[:].bitcast(I32), in_=qa_words[0].bitcast(I32))
-        nc.sync.dma_start(out=ka_codes[0][:].bitcast(I32), in_=ka_flat[:, 0:BANK])
         load_scales(nc.sync, qa_raw_scale, qa_scales)
+        nc.sync.dma_start(out=ka_codes[0][:].bitcast(I32), in_=ka_flat[:, 0:BANK])
         nc.sync.dma_start(out=qb_raw[0][:], in_=qb_rows[:, :, 0:QB_HALF])
-        nc.sync.dma_start(out=qb_raw[1][:], in_=qb_rows[:, :, QB_HALF:Q])
         load_scales(nc.sync, ka_scale, ka_scales)
+        nc.sync.dma_start(out=qb_raw[1][:], in_=qb_rows[:, :, QB_HALF:Q])
         nc.sync.dma_start(out=kb_codes[:].bitcast(I32), in_=kb_words[0].bitcast(I32))
-        load_scales(nc.sync, kb_scale, kb_scales, range(1))
+        load_scales(nc.sync, kb_scale, kb_scales)
         nc.sync.dma_start(out=ka_codes[1][:].bitcast(I32), in_=ka_flat[:, BANK:I])
+        load_weights(1)
 
         qb_dealt = qb_bf[:].rearrange("p (r m j) -> p m r j", r=PACK, j=PACK)
         half_groups = QB_HALF // PACK
@@ -101,7 +104,7 @@ def tile_mix_shares_from_two_sources_pl_kernel(
         )
         cw_bank = [ps.tile([P, BANK], F32, name="cw_bank%d" % h) for h in range(2)]
 
-        round_qb(nc.vector.tensor_copy, 0, 0, half_groups)
+        round_qb(nc.scalar.copy, 0, 0, half_groups)
         round_qb(nc.vector.tensor_copy, 1, 0, QB_VECTOR_GROUPS)
         round_qb(nc.scalar.copy, 1, QB_VECTOR_GROUPS, half_groups)
         for r in range(PACK):
@@ -110,9 +113,6 @@ def tile_mix_shares_from_two_sources_pl_kernel(
                 scales=qb_scale[:, P * r : P * (r + 1)],
                 in_=qb_bf[:, PACK * P * r : PACK * P * (r + 1)],
             )
-        nc.scalar.activation(
-            out=cw_256[:], in_=cw_rows[:].rearrange("p h m -> p (h m)"), func=ACT.Copy, scale=256.0
-        )
 
         order = [(0, 0), (1, 0), (0, 1), (2, 0), (1, 1), (3, 0), (2, 1), (3, 1)]
         acc = {}
@@ -200,14 +200,16 @@ def tile_mix_shares_from_two_sources_pl_kernel(
                 out=code_words[:, BANK * h + lo : BANK * h + hi], in_=y_codes[h][:, lo:hi].bitcast(I32)
             )
 
-        for n in range(WARM_PASSES):
-            nc.tensor.matmul_mx(
-                out=cw_bank[n % 2][:],
-                lhsT=qa_raw[:, 0 : 2 * P].bitcast(FP4X4), lhsT_scale=qa_raw_scale[:, 0:P],
-                rhs=ka_codes[0][:].bitcast(FP8X4), rhs_scale=qa_raw_scale[:],
-                start=True, stop=True,
-            )
-        for n in (0, 1, 3, 5):
+        def spread_weights(h):
+            for m in range(PACK):
+                nc.tensor.transpose(
+                    out=cw_bank[h][:].rearrange("p (n m) -> p m n", m=PACK)[:, m, :],
+                    in_=cw_256[h][:, m : m + 1].to_broadcast([P, P]),
+                    identity=ident[:],
+                )
+
+        spread_weights(0)
+        for n in (0, 1, 3):
             pass_a(n)
         pass_b(0)
         pass_b(1)
@@ -216,43 +218,37 @@ def tile_mix_shares_from_two_sources_pl_kernel(
         pass_b(3)
         pass_a(4)
         pass_b(4)
+        pass_a(5)
         pass_b(5)
         for n in range(SCORE_BANKS, 8):
             drain(n - SCORE_BANKS)
             pass_a(n)
             pass_b(n)
-        for h in range(2):
-            for m in range(PACK):
-                col = PACK * h + m
-                nc.tensor.transpose(
-                    out=cw_bank[h][:].rearrange("p (n m) -> p m n", m=PACK)[:, m, :],
-                    in_=cw_256[:, col : col + 1].to_broadcast([P, P]),
-                    identity=ident[:],
-                )
+        spread_weights(1)
         for n in range(2, 6):
             drain(n)
         invert(0)
         drain(6)
-        drain(7)
-        invert(1)
         share(0, 0)
-        invert(2)
+        invert(1)
+        drain(7)
         share(1, 0)
+        invert(2)
+        share(0, 1, 0, CHUNK)
         share(2, 0)
         invert(3)
-        share(0, 1, 0, CHUNK)
+        share(0, 1, CHUNK, BANK)
         share(3, 0, 0, CHUNK)
         round_y(nc.scalar.copy, 0)
         share(3, 0, CHUNK, BANK)
         round_y(nc.scalar.copy, 1)
-        share(0, 1, CHUNK, BANK)
         share(1, 1)
         share(2, 1)
-        share(3, 1, 0, CHUNK)
-        round_y(nc.scalar.copy, 2)
-        share(3, 1, CHUNK, BANK)
+        share(3, 1)
+        round_y(nc.scalar.copy, 2, 0, 176)
         quantize_y(0)
         round_y(nc.vector.tensor_copy, 3)
+        round_y(nc.vector.tensor_copy, 2, 176, CHUNK)
         quantize_y(1)
         store_codes(0, 0, BANK)
         quantize_y(3)

from contextlib import ExitStack

import concourse.mybir as mybir
from concourse.masks import make_identity

K, L, Q, I = 512, 512, 512, 1024
FLOPS = 2 * (K + L) * Q * I

F32 = mybir.dt.float32
BF16 = mybir.dt.bfloat16
I32 = mybir.dt.int32
U32 = mybir.dt.uint32
U8 = mybir.dt.uint8
FP8X4 = mybir.dt.float8_e4m3fn_x4
FP4X4 = mybir.dt.float4_e2m1fn_x4
ALU = mybir.AluOpType
ACT = mybir.ActivationFunctionType

P = 128
PACK = 4
BANK = 512
CHUNK = 256
SCORE_BANKS = 6
QB_HALF = Q // 2
QB_VECTOR_GROUPS = 44


def tile_mix_shares_from_two_sources_pl_kernel(
    tc, qa_words, qa_scales, ka_words, ka_scales, qb, kb_words, kb_scales, cw1, out_0, out_1, out_2
):
    nc = tc.nc
    with ExitStack() as ctx:
        sb = ctx.enter_context(tc.tile_pool(name="sb", bufs=1))
        ps = ctx.enter_context(tc.psum_pool(name="ps", bufs=1))
        ctx.enter_context(tc.manual_schedule())

        qa_raw = sb.tile([P, 2 * Q], U8, align_bytes=64)
        qa_raw_scale = sb.tile([P, Q], U8, align_bytes=64)
        qa_codes = sb.tile([P, 2 * Q], U8, align_bytes=64)
        qa_scale = sb.tile([P, Q], U8, align_bytes=64)
        ka_codes = [sb.tile([P, BANK], U32, name="ka_codes%d" % h, align_bytes=64) for h in range(2)]
        ka_scale = sb.tile([P, I], U8, align_bytes=64)
        kb_codes = sb.tile([P, 2 * I], U8, align_bytes=64)
        kb_scale = sb.tile([P, I], U8, align_bytes=64)
        qb_raw = [sb.tile([P, PACK, QB_HALF], F32, name="qb_raw%d" % u, align_bytes=64) for u in range(2)]
        qb_bf = sb.tile([P, PACK * Q], BF16, align_bytes=64)
        qb_codes = sb.tile([P, Q], U32, align_bytes=64)
        qb_scale = sb.tile([P, Q], U8, align_bytes=64)
        cw_rows = [sb.tile([P, PACK], F32, name="cw_rows%d" % h) for h in range(2)]
        cw_256 = [sb.tile([P, PACK], F32, name="cw_256_%d" % h) for h in range(2)]
        ident = sb.tile([P, P], F32)

        def load_scales(queue, plane, scales):
            for quad in range(4):
                queue.dma_start(
                    out=plane[32 * quad : 32 * quad + 4, :].bitcast(I32),
                    in_=scales[0, 4 * quad : 4 * quad + 4, :].bitcast(I32),
                )

        qb_rows = qb.rearrange("(p j) q -> p j q", j=PACK)

        ka_flat = ka_words[0].rearrange("p n t -> p (n t)").bitcast(I32)

        nc.vector.memset(qa_raw_scale[:].bitcast(I32), 0)
        nc.vector.memset(ka_scale[:].bitcast(I32), 0)
        nc.vector.memset(ident[:], 0.0)
        nc.vector.memset(kb_scale[:].bitcast(I32), 0)
        make_identity(nc, ident[:], nomemset=True)

        def load_weights(h):
            nc.sync.dma_start(
                out=cw_rows[h][:], in_=cw1[0, BANK * h : BANK * (h + 1)].rearrange("(n m) -> n m", m=PACK)
            )
            nc.gpsimd.tensor_scalar(
                out=cw_256[h][:], in0=cw_rows[h][:], scalar1=256.0, scalar2=0.0, op0=ALU.mult, op1=ALU.add
            )

        load_weights(0)
        nc.sync.dma_start(out=qa_raw[:].bitcast(I32), in_=qa_words[0].bitcast(I32))
        load_scales(nc.sync, qa_raw_scale, qa_scales)
        nc.sync.dma_start(out=ka_codes[0][:].bitcast(I32), in_=ka_flat[:, 0:BANK])
        nc.sync.dma_start(out=qb_raw[0][:], in_=qb_rows[:, :, 0:QB_HALF])
        load_scales(nc.sync, ka_scale, ka_scales)
        nc.sync.dma_start(out=qb_raw[1][:], in_=qb_rows[:, :, QB_HALF:Q])
        nc.sync.dma_start(out=kb_codes[:].bitcast(I32), in_=kb_words[0].bitcast(I32))
        load_scales(nc.sync, kb_scale, kb_scales)
        nc.sync.dma_start(out=ka_codes[1][:].bitcast(I32), in_=ka_flat[:, BANK:I])
        load_weights(1)

        qb_dealt = qb_bf[:].rearrange("p (r m j) -> p m r j", r=PACK, j=PACK)
        half_groups = QB_HALF // PACK

        def round_qb(copy, u, lo, hi):
            src = qb_raw[u][:].rearrange("p j (m r) -> p m r j", r=PACK)
            copy(out=qb_dealt[:, u * half_groups + lo : u * half_groups + hi], in_=src[:, lo:hi])

        nc.vector.tensor_copy(
            out=qa_codes[:].rearrange("p (r m b) -> p r m b", r=PACK, b=2),
            in_=qa_raw[:].rearrange("p (m r b) -> p r m b", r=PACK, b=2),
        )
        nc.vector.tensor_copy(
            out=qa_scale[:].rearrange("p (r m) -> p r m", r=PACK),
            in_=qa_raw_scale[:].rearrange("p (m r) -> p r m", r=PACK),
        )
        cw_bank = [ps.tile([P, BANK], F32, name="cw_bank%d" % h) for h in range(2)]

        round_qb(nc.scalar.copy, 0, 0, half_groups)
        round_qb(nc.vector.tensor_copy, 1, 0, QB_VECTOR_GROUPS)
        round_qb(nc.scalar.copy, 1, QB_VECTOR_GROUPS, half_groups)
        for r in range(PACK):
            nc.vector.quantize_mx(
                out=qb_codes[:, P * r : P * (r + 1)].bitcast(FP8X4),
                scales=qb_scale[:, P * r : P * (r + 1)],
                in_=qb_bf[:, PACK * P * r : PACK * P * (r + 1)],
            )

        order = [(0, 0), (1, 0), (0, 1), (2, 0), (1, 1), (3, 0), (2, 1), (3, 1)]
        acc = {}

        def pass_a(n):
            r, h = order[n]
            acc[n] = ps.tile([P, BANK], F32, name="acc%d" % n, tag="acc%d" % (n % SCORE_BANKS))
            nc.tensor.matmul_mx(
                out=acc[n][:],
                lhsT=qa_codes[:, 2 * P * r : 2 * P * (r + 1)].bitcast(FP4X4),
                lhsT_scale=qa_scale[:, P * r : P * (r + 1)],
                rhs=ka_codes[h][:].bitcast(FP8X4),
                rhs_scale=ka_scale[:, BANK * h : BANK * (h + 1)],
                start=True, stop=False,
            )

        def pass_b(n):
            r, h = order[n]
            nc.tensor.matmul_mx(
                out=acc[n][:],
                lhsT=qb_codes[:, P * r : P * (r + 1)].bitcast(FP8X4),
                lhsT_scale=qb_scale[:, P * r : P * (r + 1)],
                rhs=kb_codes[:, 2 * BANK * h : 2 * BANK * (h + 1)].bitcast(FP4X4),
                rhs_scale=kb_scale[:, BANK * h : BANK * (h + 1)],
                start=False, stop=True,
            )

        neg = [sb.tile([P, I], F32, name="neg%d" % r) for r in range(PACK)]
        expd = [sb.tile([P, I], F32, name="expd%d" % r) for r in range(PACK)]
        low_half = [sb.tile([P, 1], F32, name="low_half%d" % r) for r in range(PACK)]
        low_row = [sb.tile([P, 1], F32, name="low_row%d" % r) for r in range(PACK)]
        total = [sb.tile([P, 1], F32, name="total%d" % r) for r in range(PACK)]
        inv = [sb.tile([P, 1], F32, name="inv%d" % r) for r in range(PACK)]
        y = [sb.tile([P, PACK, BANK], F32, name="y%d" % h) for h in range(2)]
        y_bf = [sb.tile([P, PACK * CHUNK], BF16, name="y_bf%d" % c, align_bytes=64) for c in range(4)]
        y_codes = [sb.tile([P, BANK], U32, name="y_codes%d" % h, align_bytes=64) for h in range(2)]
        y_scale = sb.tile([P, I], U8, align_bytes=64)

        def drain(n):
            r, h = order[n]
            nc.vector.tensor_scalar(
                out=neg[r][:, BANK * h : BANK * (h + 1)], in0=acc[n][:],
                scalar1=-1.0, scalar2=None if h == 0 else low_half[r][:],
                op0=ALU.mult, op1=ALU.min,
                accum_out=low_half[r][:] if h == 0 else low_row[r][:],
            )
            if h == 1:
                nc.scalar.activation(
                    out=expd[r][:], in_=neg[r][:], func=ACT.Exp,
                    bias=low_row[r][:], scale=-1.0, accum_out=total[r][:],
                )

        def invert(r):
            nc.vector.reciprocal(out=inv[r][:], in_=total[r][:])

        out_rows = out_0.rearrange("(p r) i -> p r i", r=PACK)

        def share(r, h, lo=0, hi=BANK):
            nc.vector.scalar_tensor_tensor(
                out=y[h][:, r, lo:hi], in0=expd[r][:, BANK * h + lo : BANK * h + hi],
                scalar=inv[r][:], in1=cw_bank[h][:, lo:hi], op0=ALU.mult, op1=ALU.mult,
            )
            if hi == BANK:
                nc.sync.dma_start(out=out_rows[:, r, BANK * h : BANK * (h + 1)], in_=y[h][:, r, :])

        def round_y(copy, c, first=0, last=CHUNK):
            h, lo = divmod(CHUNK * c, BANK)
            copy(
                out=y_bf[c][:, PACK * first : PACK * last].rearrange("p (g i r) -> p g r i", i=4, r=PACK),
                in_=y[h][:, :, lo + first : lo + last].rearrange("p r (g i) -> p g r i", i=4),
            )

        code_words = out_1[0].rearrange("p c t -> p (c t)").bitcast(I32)

        def quantize_y(c):
            h, lo = divmod(CHUNK * c, BANK)
            nc.vector.quantize_mx(
                out=y_codes[h][:, lo : lo + CHUNK].bitcast(FP8X4),
                scales=y_scale[:, CHUNK * c : CHUNK * (c + 1)],
                in_=y_bf[c][:],
            )

        def store_codes(h, lo, hi):
            nc.sync.dma_start(
                out=code_words[:, BANK * h + lo : BANK * h + hi], in_=y_codes[h][:, lo:hi].bitcast(I32)
            )

        def spread_weights(h):
            for m in range(PACK):
                nc.tensor.transpose(
                    out=cw_bank[h][:].rearrange("p (n m) -> p m n", m=PACK)[:, m, :],
                    in_=cw_256[h][:, m : m + 1].to_broadcast([P, P]),
                    identity=ident[:],
                )

        spread_weights(0)
        for n in (0, 1, 3):
            pass_a(n)
        pass_b(0)
        pass_b(1)
        pass_a(2)
        pass_b(2)
        pass_b(3)
        pass_a(4)
        pass_b(4)
        pass_a(5)
        pass_b(5)
        for n in range(SCORE_BANKS, 8):
            drain(n - SCORE_BANKS)
            pass_a(n)
            pass_b(n)
        spread_weights(1)
        for n in range(2, 6):
            drain(n)
        invert(0)
        drain(6)
        share(0, 0)
        invert(1)
        drain(7)
        share(1, 0)
        invert(2)
        share(0, 1, 0, CHUNK)
        share(2, 0)
        invert(3)
        share(0, 1, CHUNK, BANK)
        share(3, 0, 0, CHUNK)
        round_y(nc.scalar.copy, 0)
        share(3, 0, CHUNK, BANK)
        round_y(nc.scalar.copy, 1)
        share(1, 1)
        share(2, 1)
        share(3, 1)
        round_y(nc.scalar.copy, 2, 0, 176)
        quantize_y(0)
        round_y(nc.vector.tensor_copy, 3)
        round_y(nc.vector.tensor_copy, 2, 176, CHUNK)
        quantize_y(1)
        store_codes(0, 0, BANK)
        quantize_y(3)
        store_codes(1, CHUNK, BANK)
        quantize_y(2)
        store_codes(1, 0, CHUNK)
        for quad in range(4):
            queue = nc.scalar if quad % 2 == 0 else nc.sync
            queue.dma_start(
                out=out_2[0, 4 * quad : 4 * quad + 4, :].bitcast(I32),
                in_=y_scale[32 * quad : 32 * quad + 4, :].bitcast(I32),
            )
